import numpy as np
import ml_dtypes


def mxq(x, axis, fmt="e4m3"):
    dtype, down = {"e4m3": (ml_dtypes.float8_e4m3fn, 7), "e5m2": (ml_dtypes.float8_e5m2, 14)}[fmt]
    v = np.moveaxis(np.asarray(x, np.float32).astype(ml_dtypes.bfloat16).astype(np.float64), axis, -1)
    blocks = v.reshape(v.shape[:-1] + (-1, 32))
    amax = np.abs(blocks).max(-1, keepdims=True)
    byte = np.maximum(np.where(amax > 0, np.frexp(amax)[1] - 1 + 127, 0) - down, 1)
    scale = np.exp2(byte - 127.0)
    codes = (blocks / scale).astype(np.float32).astype(dtype).astype(np.float64)
    return np.moveaxis((codes * scale).reshape(v.shape), -1, axis)


WIDE = False


def mx_kscale(k):
    if not WIDE:
        return np.ones(k)
    levels = np.array([10, -10, 5, -5, 0])
    if k % 512:
        return np.exp2(np.random.permutation(np.resize(levels, k // 32))).repeat(32)
    a = np.empty((k // 512, 16))
    for p in range(k // 512):
        a[p, :8] = np.random.permutation(np.resize(levels, 8))
        for g in range(8):
            far = levels[np.abs(levels - a[p, g]) >= 10]
            a[p, g + 8] = far[np.random.randint(len(far))]
    return np.exp2(a.ravel()).repeat(32)


def f64(x):
    return np.asarray(x).astype(np.float64)


def striped(idx):
    return np.tile(idx.reshape(-1, 16).T, (8, 1)).astype(np.uint16)


def unstriped(offs):
    return offs[:16].T.reshape(-1).astype(np.int64)


K, T, S, H, N = 1024, 2048, 1024, 512, 128


def setup_inputs():
    n = np.random.standard_normal
    s = mx_kscale(K)[:, None]
    u = mx_kscale(H)
    return {
        "xT": (n((K, T)) * s).astype(np.float32),
        "w1": (n((K, H)) / np.sqrt(K) / s * u).astype(np.float32),
        "w2": (n((H, N)) / np.sqrt(H) / u[:, None]).astype(np.float32),
        "offs": striped(np.random.permutation(T)[:S]),
    }


def reference(xT, w1, w2, offs):
    xq = mxq(f64(xT)[:, unstriped(offs)], 0, "e4m3")
    h = mxq(f64(w1), 0, "e4m3").T @ xq
    z = h - h.mean(axis=1, keepdims=True)
    return mxq(f64(w2), 0, "e4m3").T @ mxq(z, 0, "e4m3")

@@ -1,0 +1,194 @@
+from contextlib import ExitStack
+
+import concourse.mybir as mybir
+
+K, T, S, H, N = 1024, 2048, 1024, 512, 128
+FLOPS = 2 * K * H * S + 2 * H * N * S
+
+F32 = mybir.dt.float32
+BF16 = mybir.dt.bfloat16
+U32 = mybir.dt.uint32
+U16 = mybir.dt.uint16
+U8 = mybir.dt.uint8
+FP8X4 = mybir.dt.float8_e4m3fn_x4
+ACT = mybir.ActivationFunctionType
+ALU = mybir.AluOpType
+
+P = 128
+PACK = 4
+K_PASS = P * PACK
+HALF = 512
+RUN = 4
+
+X_CHUNKS = (
+    ((512, 384), (512, 384), (512, 384), (512, 320)),
+    ((512, 512), (512, 384), (512, 288), (256, 128), (128, 64), (128, 32)),
+)
+Z_PIECES = ((256, 256), (256, 0), (256, 0), (128, 0), (128, 64))
+
+
+def tile_picked_deepset_none_e_kernel(tc, xT, w1, w2, offs, out):
+    nc = tc.nc
+    with ExitStack() as ctx:
+        keep = ctx.enter_context(tc.tile_pool(name="keep", bufs=1))
+        psum = ctx.enter_context(tc.psum_pool(name="psum", bufs=1))
+
+        def sb(name, shape, dtype, tag=None):
+            return keep.tile(shape, dtype, name=name, tag=tag or name, align_bytes=64)
+
+        offsets = keep.tile([P, S // 16], U16, name="offsets")
+        x_words = [sb("x_words%d" % g, [P, T], U32) for g in range(2)]
+        x_scales = sb("x_scales", [P, T], U8)
+        nc.gpsimd.memset(x_scales[:], 0)
+
+        def load_rows(name, rows):
+            raw = sb(name, [P, PACK, rows.shape[1]], F32)
+            nc.sync.dma_start(out=raw[:], in_=rows.rearrange("(p j) c -> p j c", j=PACK))
+            return raw
+
+        def weave_views(dst, src):
+            return (dst.rearrange("p (c i) j -> p c j i", i=RUN), src.rearrange("p j (c i) -> p c j i", i=RUN))
+
+        def weave_scalar(dst, src):
+            d, s = weave_views(dst, src)
+            nc.scalar.activation(out=d, in_=s, func=ACT.Copy)
+
+        def weave_vector(dst, src):
+            d, s = weave_views(dst, src)
+            nc.vector.tensor_copy(out=d, in_=s)
+
+        def quantize(codes, scales, woven):
+            nc.vector.quantize_mx(out=codes.bitcast(FP8X4), scales=scales, in_=woven)
+
+        w1_raw = {}
+        x_raw = {}
+        for g in range(2):
+            c0 = 0
+            for n, (width, by_scalar) in enumerate(X_CHUNKS[g]):
+                x_raw[g, n] = load_rows("x_raw%d_%d" % (g, n), xT[g * K_PASS : (g + 1) * K_PASS, c0 : c0 + width])
+                c0 = c0 + width
+            if g == 0:
+                nc.sync.dma_start(offsets[:], offs)
+        w1_raw[0] = load_rows("w1_raw0", w1[0:K_PASS, :])
+        w1_raw[1] = load_rows("w1_raw1", w1[K_PASS : 2 * K_PASS, :])
+        w2_raw = load_rows("w2_raw", w2)
+
+        w1_codes = {}
+        w1_scales = {}
+
+        def prepare_w1(g, u):
+            woven = sb("w1_woven%d_%d" % (g, u), [P, 2, P, PACK], BF16)
+            src = w1_raw[g][:].rearrange("p j (m t) -> p m j t", t=PACK)[:, :, :, 2 * u : 2 * u + 2]
+            nc.scalar.activation(out=woven[:].rearrange("p t m j -> p m j t"), in_=src, func=ACT.Copy)
+            w1_codes[g, u] = sb("w1_codes%d_%d" % (g, u), [P, 2 * P], U32)
+            w1_scales[g, u] = sb("w1_scales%d_%d" % (g, u), [P, 2 * P], U8)
+            quantize(w1_codes[g, u][:], w1_scales[g, u][:], woven[:].rearrange("p t m j -> p (t m j)"))
+
+        def quantize_x(g):
+            c0 = 0
+            for n, (width, by_scalar) in enumerate(X_CHUNKS[g]):
+                woven = sb("x_woven%d_%d" % (g, n), [P, width, PACK], BF16)
+                raw = x_raw[g, n]
+                weave_scalar(woven[:, 0:by_scalar, :], raw[:, :, 0:by_scalar])
+                if by_scalar < width:
+                    weave_vector(woven[:, by_scalar:width, :], raw[:, :, by_scalar:width])
+                quantize(
+                    x_words[g][:, c0 : c0 + width],
+                    x_scales[PACK * g : P, c0 : c0 + width],
+                    woven[:].rearrange("p c j -> p (c j)"),
+                )
+                c0 = c0 + width
+
+        def gather(name, window, dtype, half, tag=None):
+            picked = sb(name, [P, HALF], dtype, tag)
+            cols = slice(half * HALF // 16, (half + 1) * HALF // 16)
+            nc.vector.tensor_copy(out=picked[:], in_=window[:].indirect(offsets[:, cols]))
+            return picked
+
+        quantize_x(0)
+        picked_words = {}
+        picked_scales = {}
+        for half in range(2):
+            picked_words[0, half] = gather("picked_words0_%d" % half, x_words[0], U32, half)
+        quantize_x(1)
+        for half in range(2):
+            picked_scales[half] = gather("picked_scales%d" % half, x_scales, U8, half)
+        for half in range(2):
+            prepare_w1(0, half)
+            picked_words[1, half] = gather("picked_words1_%d" % half, x_words[1], U32, half, "w1_woven0_%d" % half)
+        prepare_w1(1, 0)
+        prepare_w1(1, 1)
+
+        banks = {}
+        for half in range(2):
+            for t in range(PACK):
+                banks[t, half] = psum.tile([P, HALF], F32, name="bank%d_%d" % (t, half), tag="bank%d_%d" % (t, half))
+
+        def first_layer(g, t, half):
+            cols = slice((t % 2) * P, (t % 2 + 1) * P)
+            nc.tensor.matmul_mx(
+                out=banks[t, half][:],
+                lhsT=w1_codes[g, t // 2][:, cols].bitcast(FP8X4),
+                lhsT_scale=w1_scales[g, t // 2][:, cols],
+                rhs=picked_words[g, half][:].bitcast(FP8X4),
+                rhs_scale=picked_scales[half][PACK * g : P, :],
+                start=(g == 0),
+                stop=(g == 1),
+            )
+
+        for t in range(PACK):
+            for half in range(2):
+                first_layer(0, t, half)
+        for t in range(PACK):
+            for half in range(2):
+                first_layer(1, t, half)
+
+        w2_woven = sb("w2_woven", [P, N, PACK], BF16)
+        weave_scalar(w2_woven[:], w2_raw[:])
+        w2_codes = sb("w2_codes", [P, N], U32)
+        w2_scales = sb("w2_scales", [P, N], U8)
+        quantize(w2_codes[:], w2_scales[:], w2_woven[:].rearrange("p c j -> p (c j)"))
+
+        h = [sb("h0", [P, PACK, HALF], F32, "w1_woven1_1"), sb("h1", [P, PACK, HALF], F32)]
+        sums = [sb("sums%d" % half, [P, PACK], F32) for half in range(2)]
+        minus_mean = sb("minus_mean", [P, PACK, 8], F32)
+        for t in range(PACK):
+            nc.vector.tensor_scalar(
+                out=h[0][:, t, :], in0=banks[t, 0][:], scalar1=1.0, scalar2=None,
+                op0=ALU.mult, op1=ALU.add, accum_out=sums[0][:, t : t + 1],
+            )
+            nc.scalar.activation(out=h[1][:, t, :], in_=banks[t, 1][:], func=ACT.Copy, accum_out=sums[1][:, t : t + 1])
+            (nc.vector if t == PACK - 1 else nc.gpsimd).tensor_scalar(
+                out=minus_mean[:, t, 0:1], in0=sums[0][:, t : t + 1], scalar1=sums[1][:, t : t + 1],
+                scalar2=-1.0 / S, op0=ALU.add, op1=ALU.mult,
+            )
+
+        c0 = 0
+        for n, (width, fused) in enumerate(Z_PIECES):
+            src = h[c0 // HALF]
+            a = c0 % HALF
+            z_woven = sb("z_woven%d" % n, [P, width, PACK], BF16)
+            if fused:
+                d, s = weave_views(z_woven[:, 0:fused, :], src[:, :, a : a + fused])
+                m = minus_mean[:, :, 0:1].unsqueeze(1).to_broadcast([P, fused // RUN, PACK, RUN])
+                nc.vector.tensor_tensor(out=d, in0=s, in1=m, op=ALU.add)
+            if fused < width:
+                z_rows = sb("z_rows%d" % n, [P, PACK, width - fused], BF16)
+                for t in range(PACK):
+                    nc.scalar.activation(
+                        out=z_rows[:, t, :], in_=src[:, t, a + fused : a + width], func=ACT.Identity,
+                        bias=minus_mean[:, t, 0:1],
+                    )
+                weave_vector(z_woven[:, fused:width, :], z_rows[:])
+            z_codes = sb("z_codes%d" % n, [P, width], U32)
+            z_scales = sb("z_scales%d" % n, [P, width], U8)
+            quantize(z_codes[:], z_scales[:], z_woven[:].rearrange("p c j -> p (c j)"))
+            acc = psum.tile([P, HALF], F32, name="acc%d" % n, tag="bank%d_%d" % (n % PACK, n // PACK))
+            nc.tensor.matmul_mx(
+                out=acc[:, 0:width], lhsT=w2_codes[:].bitcast(FP8X4), lhsT_scale=w2_scales[:],
+                rhs=z_codes[:].bitcast(FP8X4), rhs_scale=z_scales[:], start=True, stop=True,
+            )
+            result = sb("result%d" % n, [P, width], F32)
+            nc.scalar.copy(out=result[:], in_=acc[:, 0:width])
+            nc.sync.dma_start(out=out[:, c0 : c0 + width], in_=result[:])
+            c0 = c0 + width

@@ -20,11 +20,12 @@ K_PASS = P * PACK
 HALF = 512
 RUN = 4
 
-X_CHUNKS = (
-    ((512, 384), (512, 384), (512, 384), (512, 320)),
-    ((512, 512), (512, 384), (512, 288), (256, 128), (128, 64), (128, 32)),
+X_LOADS = (
+    (((512, 256), (512, 256)), ((512, 384),), ((512, 224),)),
+    (((512, 256), (512, 192)), ((512, 288),), ((256, 160),), ((256, 112),)),
 )
-Z_PIECES = ((256, 256), (256, 0), (256, 0), (128, 0), (128, 64))
+Z_PIECES = ((256, 2), (256, 2), (256, 3), (128, 3), (128, 3))
+WARM_UP = 3
 
 
 def tile_picked_deepset_none_e_kernel(tc, xT, w1, w2, offs, out):
@@ -64,7 +65,8 @@ def tile_picked_deepset_none_e_kernel(tc, xT, w1, w2, offs, out):
         x_raw = {}
         for g in range(2):
             c0 = 0
-            for n, (width, by_scalar) in enumerate(X_CHUNKS[g]):
+            for n, pieces in enumerate(X_LOADS[g]):
+                width = sum(piece[0] for piece in pieces)
                 x_raw[g, n] = load_rows("x_raw%d_%d" % (g, n), xT[g * K_PASS : (g + 1) * K_PASS, c0 : c0 + width])
                 c0 = c0 + width
             if g == 0:
@@ -86,18 +88,22 @@ def tile_picked_deepset_none_e_kernel(tc, xT, w1, w2, offs, out):
 
         def quantize_x(g):
             c0 = 0
-            for n, (width, by_scalar) in enumerate(X_CHUNKS[g]):
-                woven = sb("x_woven%d_%d" % (g, n), [P, width, PACK], BF16)
+            for n, pieces in enumerate(X_LOADS[g]):
                 raw = x_raw[g, n]
-                weave_scalar(woven[:, 0:by_scalar, :], raw[:, :, 0:by_scalar])
-                if by_scalar < width:
-                    weave_vector(woven[:, by_scalar:width, :], raw[:, :, by_scalar:width])
-                quantize(
-                    x_words[g][:, c0 : c0 + width],
-                    x_scales[PACK * g : P, c0 : c0 + width],
-                    woven[:].rearrange("p c j -> p (c j)"),
-                )
-                c0 = c0 + width
+                a = 0
+                for width, by_scalar in pieces:
+                    woven = sb("x_woven%d_%d" % (g, c0), [P, width, PACK], BF16)
+                    if by_scalar > 0:
+                        weave_scalar(woven[:, 0:by_scalar, :], raw[:, :, a : a + by_scalar])
+                    if by_scalar < width:
+                        weave_vector(woven[:, by_scalar:width, :], raw[:, :, a + by_scalar : a + width])
+                    quantize(
+                        x_words[g][:, c0 : c0 + width],
+                        x_scales[PACK * g : P, c0 : c0 + width],
+                        woven[:].rearrange("p c j -> p (c j)"),
+                    )
+                    a = a + width
+                    c0 = c0 + width
 
         def gather(name, window, dtype, half, tag=None):
             picked = sb(name, [P, HALF], dtype, tag)
@@ -119,6 +125,17 @@ def tile_picked_deepset_none_e_kernel(tc, xT, w1, w2, offs, out):
         prepare_w1(1, 0)
         prepare_w1(1, 1)
 
+        warm = psum.tile([P, HALF], F32, name="warm", tag="bank3_1")
+        for n in range(WARM_UP):
+            nc.tensor.matmul_mx(
+                out=warm[:],
+                lhsT=picked_words[0, 0][:, 0:P].bitcast(FP8X4),
+                lhsT_scale=picked_scales[0][:, 0:P],
+                rhs=picked_words[0, 0][:].bitcast(FP8X4),
+                rhs_scale=picked_scales[0][:],
+                start=True,
+                stop=True,
+            )
         banks = {}
         for half in range(2):
             for t in range(PACK):
@@ -143,12 +160,6 @@ def tile_picked_deepset_none_e_kernel(tc, xT, w1, w2, offs, out):
             for half in range(2):
                 first_layer(1, t, half)
 
-        w2_woven = sb("w2_woven", [P, N, PACK], BF16)
-        weave_scalar(w2_woven[:], w2_raw[:])
-        w2_codes = sb("w2_codes", [P, N], U32)
-        w2_scales = sb("w2_scales", [P, N], U8)
-        quantize(w2_codes[:], w2_scales[:], w2_woven[:].rearrange("p c j -> p (c j)"))
-
         h = [sb("h0", [P, PACK, HALF], F32, "w1_woven1_1"), sb("h1", [P, PACK, HALF], F32)]
         sums = [sb("sums%d" % half, [P, PACK], F32) for half in range(2)]
         minus_mean = sb("minus_mean", [P, PACK, 8], F32)
@@ -163,23 +174,30 @@ def tile_picked_deepset_none_e_kernel(tc, xT, w1, w2, offs, out):
                 scalar2=-1.0 / S, op0=ALU.add, op1=ALU.mult,
             )
 
+        w2_woven = sb("w2_woven", [P, N, PACK], BF16)
+        weave_scalar(w2_woven[:], w2_raw[:])
+        w2_codes = sb("w2_codes", [P, N], U32)
+        w2_scales = sb("w2_scales", [P, N], U8)
+        quantize(w2_codes[:], w2_scales[:], w2_woven[:].rearrange("p c j -> p (c j)"))
+
         c0 = 0
-        for n, (width, fused) in enumerate(Z_PIECES):
+        for n, (width, by_scalar) in enumerate(Z_PIECES):
             src = h[c0 // HALF]
             a = c0 % HALF
-            z_woven = sb("z_woven%d" % n, [P, width, PACK], BF16)
-            if fused:
-                d, s = weave_views(z_woven[:, 0:fused, :], src[:, :, a : a + fused])
-                m = minus_mean[:, :, 0:1].unsqueeze(1).to_broadcast([P, fused // RUN, PACK, RUN])
-                nc.vector.tensor_tensor(out=d, in0=s, in1=m, op=ALU.add)
-            if fused < width:
-                z_rows = sb("z_rows%d" % n, [P, PACK, width - fused], BF16)
-                for t in range(PACK):
+            z_rows = sb("z_rows%d" % n, [P, PACK, width], BF16)
+            for t in range(PACK):
+                if t < by_scalar:
                     nc.scalar.activation(
-                        out=z_rows[:, t, :], in_=src[:, t, a + fused : a + width], func=ACT.Identity,
+                        out=z_rows[:, t, :], in_=src[:, t, a : a + width], func=ACT.Identity,
                         bias=minus_mean[:, t, 0:1],
                     )
-                weave_vector(z_woven[:, fused:width, :], z_rows[:])
+                else:
+                    nc.vector.tensor_scalar(
+                        out=z_rows[:, t, :], in0=src[:, t, a : a + width], scalar1=minus_mean[:, t, 0:1],
+                        scalar2=None, op0=ALU.add,
+                    )
+            z_woven = sb("z_woven%d" % n, [P, width, PACK], BF16)
+            weave_vector(z_woven[:], z_rows[:])
             z_codes = sb("z_codes%d" % n, [P, width], U32)
             z_scales = sb("z_scales%d" % n, [P, width], U8)
             quantize(z_codes[:], z_scales[:], z_woven[:].rearrange("p c j -> p (c j)"))
@@ -189,6 +207,9 @@ def tile_picked_deepset_none_e_kernel(tc, xT, w1, w2, offs, out):
                 rhs=z_codes[:].bitcast(FP8X4), rhs_scale=z_scales[:], start=True, stop=True,
             )
             result = sb("result%d" % n, [P, width], F32)
-            nc.scalar.copy(out=result[:], in_=acc[:, 0:width])
+            if n == len(Z_PIECES) - 1:
+                nc.vector.tensor_copy(out=result[:], in_=acc[:, 0:width])
+            else:
+                nc.scalar.copy(out=result[:], in_=acc[:, 0:width])
             nc.sync.dma_start(out=out[:, c0 : c0 + width], in_=result[:])
             c0 = c0 + width

@@ -17,7 +17,9 @@ ALU = mybir.AluOpType
 P = 128
 PACK = 4
 K_PASS = P * PACK
-HALF = 512
+PASSES = K // K_PASS
+HALF = S // 2
+LIST_ROWS = 16
 RUN = 4
 
 X_LOADS = (
@@ -25,7 +27,7 @@ X_LOADS = (
     (((512, 256), (512, 192)), ((512, 288),), ((256, 160),), ((256, 112),)),
 )
 Z_PIECES = ((256, 2), (256, 2), (256, 3), (128, 3), (128, 3))
-WARM_UP = 3
+MEAN_PITCH = 8
 
 
 def tile_picked_deepset_none_e_kernel(tc, xT, w1, w2, offs, out):
@@ -34,123 +36,107 @@ def tile_picked_deepset_none_e_kernel(tc, xT, w1, w2, offs, out):
         keep = ctx.enter_context(tc.tile_pool(name="keep", bufs=1))
         psum = ctx.enter_context(tc.psum_pool(name="psum", bufs=1))
 
-        def sb(name, shape, dtype, tag=None):
-            return keep.tile(shape, dtype, name=name, tag=tag or name, align_bytes=64)
+        def sbuf(name, shape, dtype, after=None):
+            return keep.tile(shape, dtype, name=name, tag=after or name, align_bytes=64)
 
-        offsets = keep.tile([P, S // 16], U16, name="offsets")
-        x_words = [sb("x_words%d" % g, [P, T], U32) for g in range(2)]
-        x_scales = sb("x_scales", [P, T], U8)
-        nc.gpsimd.memset(x_scales[:], 0)
-
-        def load_rows(name, rows):
-            raw = sb(name, [P, PACK, rows.shape[1]], F32)
+        def load_pass(name, rows):
+            raw = sbuf(name, [P, PACK, rows.shape[1]], F32)
             nc.sync.dma_start(out=raw[:], in_=rows.rearrange("(p j) c -> p j c", j=PACK))
             return raw
 
-        def weave_views(dst, src):
-            return (dst.rearrange("p (c i) j -> p c j i", i=RUN), src.rearrange("p j (c i) -> p c j i", i=RUN))
+        def weave_views(woven, rows):
+            return woven.rearrange("p (c i) j -> p c j i", i=RUN), rows.rearrange("p j (c i) -> p c j i", i=RUN)
 
-        def weave_scalar(dst, src):
-            d, s = weave_views(dst, src)
-            nc.scalar.activation(out=d, in_=s, func=ACT.Copy)
+        def weave_on_scalar(woven, rows):
+            dst, src = weave_views(woven, rows)
+            nc.scalar.activation(out=dst, in_=src, func=ACT.Copy)
 
-        def weave_vector(dst, src):
-            d, s = weave_views(dst, src)
-            nc.vector.tensor_copy(out=d, in_=s)
+        def weave_on_vector(woven, rows):
+            dst, src = weave_views(woven, rows)
+            nc.vector.tensor_copy(out=dst, in_=src)
 
         def quantize(codes, scales, woven):
-            nc.vector.quantize_mx(out=codes.bitcast(FP8X4), scales=scales, in_=woven)
+            nc.vector.quantize_mx(out=codes.bitcast(FP8X4), scales=scales, in_=woven.rearrange("p c j -> p (c j)"))
 
-        w1_raw = {}
+        offsets = keep.tile([P, S // LIST_ROWS], U16, name="offsets")
+        x_words = [sbuf("x_words%d" % g, [P, T], U32) for g in range(PASSES)]
+        x_scales = sbuf("x_scales", [P, T], U8)
+        nc.gpsimd.memset(x_scales[:], 0)
+
         x_raw = {}
-        for g in range(2):
-            c0 = 0
+        for g in range(PASSES):
+            first = 0
             for n, pieces in enumerate(X_LOADS[g]):
-                width = sum(piece[0] for piece in pieces)
-                x_raw[g, n] = load_rows("x_raw%d_%d" % (g, n), xT[g * K_PASS : (g + 1) * K_PASS, c0 : c0 + width])
-                c0 = c0 + width
+                width = sum(members for members, on_scalar in pieces)
+                rows = xT[g * K_PASS : (g + 1) * K_PASS, first : first + width]
+                x_raw[g, n] = load_pass("x_raw%d_%d" % (g, n), rows)
+                first = first + width
             if g == 0:
                 nc.sync.dma_start(offsets[:], offs)
-        w1_raw[0] = load_rows("w1_raw0", w1[0:K_PASS, :])
-        w1_raw[1] = load_rows("w1_raw1", w1[K_PASS : 2 * K_PASS, :])
-        w2_raw = load_rows("w2_raw", w2)
+        w1_raw = [load_pass("w1_raw%d" % g, w1[g * K_PASS : (g + 1) * K_PASS, :]) for g in range(PASSES)]
+        w2_raw = load_pass("w2_raw", w2)
+
+        def quantize_x(g):
+            first = 0
+            for n, pieces in enumerate(X_LOADS[g]):
+                raw = x_raw[g, n]
+                start = 0
+                for members, on_scalar in pieces:
+                    woven = sbuf("x_woven%d_%d" % (g, first), [P, members, PACK], BF16)
+                    weave_on_scalar(woven[:, 0:on_scalar, :], raw[:, :, start : start + on_scalar])
+                    weave_on_vector(woven[:, on_scalar:members, :], raw[:, :, start + on_scalar : start + members])
+                    columns = slice(first, first + members)
+                    quantize(x_words[g][:, columns], x_scales[PACK * g : P, columns], woven[:])
+                    start = start + members
+                    first = first + members
+
+        def gather(name, window, dtype, half, after=None):
+            picked = sbuf(name, [P, HALF], dtype, after)
+            columns = slice(half * HALF // LIST_ROWS, (half + 1) * HALF // LIST_ROWS)
+            nc.vector.tensor_copy(out=picked[:], in_=window[:].indirect(offsets[:, columns]))
+            return picked
 
         w1_codes = {}
         w1_scales = {}
 
-        def prepare_w1(g, u):
-            woven = sb("w1_woven%d_%d" % (g, u), [P, 2, P, PACK], BF16)
+        def quantize_w1(g, u):
+            woven = sbuf("w1_woven%d_%d" % (g, u), [P, 2 * P, PACK], BF16)
+            dst = woven[:].rearrange("p (t m) j -> p m j t", t=2)
             src = w1_raw[g][:].rearrange("p j (m t) -> p m j t", t=PACK)[:, :, :, 2 * u : 2 * u + 2]
-            nc.scalar.activation(out=woven[:].rearrange("p t m j -> p m j t"), in_=src, func=ACT.Copy)
-            w1_codes[g, u] = sb("w1_codes%d_%d" % (g, u), [P, 2 * P], U32)
-            w1_scales[g, u] = sb("w1_scales%d_%d" % (g, u), [P, 2 * P], U8)
-            quantize(w1_codes[g, u][:], w1_scales[g, u][:], woven[:].rearrange("p t m j -> p (t m j)"))
+            nc.scalar.activation(out=dst, in_=src, func=ACT.Copy)
+            w1_codes[g, u] = sbuf("w1_codes%d_%d" % (g, u), [P, 2 * P], U32)
+            w1_scales[g, u] = sbuf("w1_scales%d_%d" % (g, u), [P, 2 * P], U8)
+            quantize(w1_codes[g, u][:], w1_scales[g, u][:], woven[:])
 
-        def quantize_x(g):
-            c0 = 0
-            for n, pieces in enumerate(X_LOADS[g]):
-                raw = x_raw[g, n]
-                a = 0
-                for width, by_scalar in pieces:
-                    woven = sb("x_woven%d_%d" % (g, c0), [P, width, PACK], BF16)
-                    if by_scalar > 0:
-                        weave_scalar(woven[:, 0:by_scalar, :], raw[:, :, a : a + by_scalar])
-                    if by_scalar < width:
-                        weave_vector(woven[:, by_scalar:width, :], raw[:, :, a + by_scalar : a + width])
-                    quantize(
-                        x_words[g][:, c0 : c0 + width],
-                        x_scales[PACK * g : P, c0 : c0 + width],
-                        woven[:].rearrange("p c j -> p (c j)"),
-                    )
-                    a = a + width
-                    c0 = c0 + width
-
-        def gather(name, window, dtype, half, tag=None):
-            picked = sb(name, [P, HALF], dtype, tag)
-            cols = slice(half * HALF // 16, (half + 1) * HALF // 16)
-            nc.vector.tensor_copy(out=picked[:], in_=window[:].indirect(offsets[:, cols]))
-            return picked
-
-        quantize_x(0)
         picked_words = {}
         picked_scales = {}
+        quantize_x(0)
         for half in range(2):
             picked_words[0, half] = gather("picked_words0_%d" % half, x_words[0], U32, half)
         quantize_x(1)
         for half in range(2):
             picked_scales[half] = gather("picked_scales%d" % half, x_scales, U8, half)
         for half in range(2):
-            prepare_w1(0, half)
+            quantize_w1(0, half)
             picked_words[1, half] = gather("picked_words1_%d" % half, x_words[1], U32, half, "w1_woven0_%d" % half)
-        prepare_w1(1, 0)
-        prepare_w1(1, 1)
+        for u in range(2):
+            quantize_w1(1, u)
 
-        warm = psum.tile([P, HALF], F32, name="warm", tag="bank3_1")
-        for n in range(WARM_UP):
-            nc.tensor.matmul_mx(
-                out=warm[:],
-                lhsT=picked_words[0, 0][:, 0:P].bitcast(FP8X4),
-                lhsT_scale=picked_scales[0][:, 0:P],
-                rhs=picked_words[0, 0][:].bitcast(FP8X4),
-                rhs_scale=picked_scales[0][:],
-                start=True,
-                stop=True,
-            )
         banks = {}
         for half in range(2):
             for t in range(PACK):
                 banks[t, half] = psum.tile([P, HALF], F32, name="bank%d_%d" % (t, half), tag="bank%d_%d" % (t, half))
 
         def first_layer(g, t, half):
-            cols = slice((t % 2) * P, (t % 2 + 1) * P)
+            columns = slice((t % 2) * P, (t % 2 + 1) * P)
             nc.tensor.matmul_mx(
                 out=banks[t, half][:],
-                lhsT=w1_codes[g, t // 2][:, cols].bitcast(FP8X4),
-                lhsT_scale=w1_scales[g, t // 2][:, cols],
+                lhsT=w1_codes[g, t // 2][:, columns].bitcast(FP8X4),
+                lhsT_scale=w1_scales[g, t // 2][:, columns],
                 rhs=picked_words[g, half][:].bitcast(FP8X4),
                 rhs_scale=picked_scales[half][PACK * g : P, :],
                 start=(g == 0),
-                stop=(g == 1),
+                stop=(g == PASSES - 1),
             )
 
         for t in range(PACK):
@@ -160,56 +146,56 @@ def tile_picked_deepset_none_e_kernel(tc, xT, w1, w2, offs, out):
             for half in range(2):
                 first_layer(1, t, half)
 
-        h = [sb("h0", [P, PACK, HALF], F32, "w1_woven1_1"), sb("h1", [P, PACK, HALF], F32)]
-        sums = [sb("sums%d" % half, [P, PACK], F32) for half in range(2)]
-        minus_mean = sb("minus_mean", [P, PACK, 8], F32)
+        h = [sbuf("h0", [P, PACK, HALF], F32, "w1_woven1_1"), sbuf("h1", [P, PACK, HALF], F32)]
+        sums = [sbuf("sums%d" % half, [P, PACK], F32) for half in range(2)]
+        minus_mean = sbuf("minus_mean", [P, PACK, MEAN_PITCH], F32)
         for t in range(PACK):
             nc.vector.tensor_scalar(
                 out=h[0][:, t, :], in0=banks[t, 0][:], scalar1=1.0, scalar2=None,
                 op0=ALU.mult, op1=ALU.add, accum_out=sums[0][:, t : t + 1],
             )
-            nc.scalar.activation(out=h[1][:, t, :], in_=banks[t, 1][:], func=ACT.Copy, accum_out=sums[1][:, t : t + 1])
-            (nc.vector if t == PACK - 1 else nc.gpsimd).tensor_scalar(
+            nc.scalar.activation(
+                out=h[1][:, t, :], in_=banks[t, 1][:], func=ACT.Copy, accum_out=sums[1][:, t : t + 1]
+            )
+            joiner = nc.vector if t == PACK - 1 else nc.gpsimd
+            joiner.tensor_scalar(
                 out=minus_mean[:, t, 0:1], in0=sums[0][:, t : t + 1], scalar1=sums[1][:, t : t + 1],
                 scalar2=-1.0 / S, op0=ALU.add, op1=ALU.mult,
             )
 
-        w2_woven = sb("w2_woven", [P, N, PACK], BF16)
-        weave_scalar(w2_woven[:], w2_raw[:])
-        w2_codes = sb("w2_codes", [P, N], U32)
-        w2_scales = sb("w2_scales", [P, N], U8)
-        quantize(w2_codes[:], w2_scales[:], w2_woven[:].rearrange("p c j -> p (c j)"))
+        w2_woven = sbuf("w2_woven", [P, N, PACK], BF16)
+        weave_on_scalar(w2_woven[:], w2_raw[:])
+        w2_codes = sbuf("w2_codes", [P, N], U32)
+        w2_scales = sbuf("w2_scales", [P, N], U8)
+        quantize(w2_codes[:], w2_scales[:], w2_woven[:])
 
-        c0 = 0
-        for n, (width, by_scalar) in enumerate(Z_PIECES):
-            src = h[c0 // HALF]
-            a = c0 % HALF
-            z_rows = sb("z_rows%d" % n, [P, PACK, width], BF16)
-            for t in range(PACK):
-                if t < by_scalar:
-                    nc.scalar.activation(
-                        out=z_rows[:, t, :], in_=src[:, t, a : a + width], func=ACT.Identity,
-                        bias=minus_mean[:, t, 0:1],
-                    )
-                else:
-                    nc.vector.tensor_scalar(
-                        out=z_rows[:, t, :], in0=src[:, t, a : a + width], scalar1=minus_mean[:, t, 0:1],
-                        scalar2=None, op0=ALU.add,
-                    )
-            z_woven = sb("z_woven%d" % n, [P, width, PACK], BF16)
-            weave_vector(z_woven[:], z_rows[:])
-            z_codes = sb("z_codes%d" % n, [P, width], U32)
-            z_scales = sb("z_scales%d" % n, [P, width], U8)
-            quantize(z_codes[:], z_scales[:], z_woven[:].rearrange("p c j -> p (c j)"))
-            acc = psum.tile([P, HALF], F32, name="acc%d" % n, tag="bank%d_%d" % (n % PACK, n // PACK))
+        first = 0
+        for n, (width, tiles_on_scalar) in enumerate(Z_PIECES):
+            source = h[first // HALF][:, :, first % HALF : first % HALF + width]
+            z_rows = sbuf("z_rows%d" % n, [P, PACK, width], BF16)
+            for t in range(tiles_on_scalar):
+                nc.scalar.activation(
+                    out=z_rows[:, t, :], in_=source[:, t, :], func=ACT.Identity, bias=minus_mean[:, t, 0:1]
+                )
+            for t in range(tiles_on_scalar, PACK):
+                nc.vector.tensor_scalar(
+                    out=z_rows[:, t, :], in0=source[:, t, :], scalar1=minus_mean[:, t, 0:1], scalar2=None,
+                    op0=ALU.add,
+                )
+            z_woven = sbuf("z_woven%d" % n, [P, width, PACK], BF16)
+            weave_on_vector(z_woven[:], z_rows[:])
+            z_codes = sbuf("z_codes%d" % n, [P, width], U32)
+            z_scales = sbuf("z_scales%d" % n, [P, width], U8)
+            quantize(z_codes[:], z_scales[:], z_woven[:])
+            product = psum.tile([P, HALF], F32, name="acc%d" % n, tag="bank%d_%d" % (n % PACK, n // PACK))
             nc.tensor.matmul_mx(
-                out=acc[:, 0:width], lhsT=w2_codes[:].bitcast(FP8X4), lhsT_scale=w2_scales[:],
+                out=product[:, 0:width], lhsT=w2_codes[:].bitcast(FP8X4), lhsT_scale=w2_scales[:],
                 rhs=z_codes[:].bitcast(FP8X4), rhs_scale=z_scales[:], start=True, stop=True,
             )
-            result = sb("result%d" % n, [P, width], F32)
+            result = sbuf("result%d" % n, [P, width], F32)
             if n == len(Z_PIECES) - 1:
-                nc.vector.tensor_copy(out=result[:], in_=acc[:, 0:width])
+                nc.vector.tensor_copy(out=result[:], in_=product[:, 0:width])
             else:
-                nc.scalar.copy(out=result[:], in_=acc[:, 0:width])
-            nc.sync.dma_start(out=out[:, c0 : c0 + width], in_=result[:])
-            c0 = c0 + width
+                nc.scalar.copy(out=result[:], in_=product[:, 0:width])
+            nc.sync.dma_start(out=out[:, first : first + width], in_=result[:])
+            first = first + width

from contextlib import ExitStack

import concourse.mybir as mybir

K, T, S, H, N = 1024, 2048, 1024, 512, 128
FLOPS = 2 * K * H * S + 2 * H * N * S

F32 = mybir.dt.float32
BF16 = mybir.dt.bfloat16
U32 = mybir.dt.uint32
U16 = mybir.dt.uint16
U8 = mybir.dt.uint8
FP8X4 = mybir.dt.float8_e4m3fn_x4
ACT = mybir.ActivationFunctionType
ALU = mybir.AluOpType

P = 128
PACK = 4
K_PASS = P * PACK
PASSES = K // K_PASS
HALF = S // 2
LIST_ROWS = 16
RUN = 4

X_LOADS = (
    (((512, 256), (512, 256)), ((512, 384),), ((512, 224),)),
    (((512, 256), (512, 192)), ((512, 288),), ((256, 160),), ((256, 112),)),
)
Z_PIECES = ((256, 2), (256, 2), (256, 3), (128, 3), (128, 3))
MEAN_PITCH = 8


def tile_picked_deepset_none_e_kernel(tc, xT, w1, w2, offs, out):
    nc = tc.nc
    with ExitStack() as ctx:
        keep = ctx.enter_context(tc.tile_pool(name="keep", bufs=1))
        psum = ctx.enter_context(tc.psum_pool(name="psum", bufs=1))

        def sbuf(name, shape, dtype, after=None):
            return keep.tile(shape, dtype, name=name, tag=after or name, align_bytes=64)

        def load_pass(name, rows):
            raw = sbuf(name, [P, PACK, rows.shape[1]], F32)
            nc.sync.dma_start(out=raw[:], in_=rows.rearrange("(p j) c -> p j c", j=PACK))
            return raw

        def weave_views(woven, rows):
            return woven.rearrange("p (c i) j -> p c j i", i=RUN), rows.rearrange("p j (c i) -> p c j i", i=RUN)

        def weave_on_scalar(woven, rows):
            dst, src = weave_views(woven, rows)
            nc.scalar.activation(out=dst, in_=src, func=ACT.Copy)

        def weave_on_vector(woven, rows):
            dst, src = weave_views(woven, rows)
            nc.vector.tensor_copy(out=dst, in_=src)

        def quantize(codes, scales, woven):
            nc.vector.quantize_mx(out=codes.bitcast(FP8X4), scales=scales, in_=woven.rearrange("p c j -> p (c j)"))

        offsets = keep.tile([P, S // LIST_ROWS], U16, name="offsets")
        x_words = [sbuf("x_words%d" % g, [P, T], U32) for g in range(PASSES)]
        x_scales = sbuf("x_scales", [P, T], U8)
        nc.gpsimd.memset(x_scales[:], 0)

        x_raw = {}
        for g in range(PASSES):
            first = 0
            for n, pieces in enumerate(X_LOADS[g]):
                width = sum(members for members, on_scalar in pieces)
                rows = xT[g * K_PASS : (g + 1) * K_PASS, first : first + width]
                x_raw[g, n] = load_pass("x_raw%d_%d" % (g, n), rows)
                first = first + width
            if g == 0:
                nc.sync.dma_start(offsets[:], offs)
        w1_raw = [load_pass("w1_raw%d" % g, w1[g * K_PASS : (g + 1) * K_PASS, :]) for g in range(PASSES)]
        w2_raw = load_pass("w2_raw", w2)

        def quantize_x(g):
            first = 0
            for n, pieces in enumerate(X_LOADS[g]):
                raw = x_raw[g, n]
                start = 0
                for members, on_scalar in pieces:
                    woven = sbuf("x_woven%d_%d" % (g, first), [P, members, PACK], BF16)
                    weave_on_scalar(woven[:, 0:on_scalar, :], raw[:, :, start : start + on_scalar])
                    weave_on_vector(woven[:, on_scalar:members, :], raw[:, :, start + on_scalar : start + members])
                    columns = slice(first, first + members)
                    quantize(x_words[g][:, columns], x_scales[PACK * g : P, columns], woven[:])
                    start = start + members
                    first = first + members

        def gather(name, window, dtype, half, after=None):
            picked = sbuf(name, [P, HALF], dtype, after)
            columns = slice(half * HALF // LIST_ROWS, (half + 1) * HALF // LIST_ROWS)
            nc.vector.tensor_copy(out=picked[:], in_=window[:].indirect(offsets[:, columns]))
            return picked

        w1_codes = {}
        w1_scales = {}

        def quantize_w1(g, u):
            woven = sbuf("w1_woven%d_%d" % (g, u), [P, 2 * P, PACK], BF16)
            dst = woven[:].rearrange("p (t m) j -> p m j t", t=2)
            src = w1_raw[g][:].rearrange("p j (m t) -> p m j t", t=PACK)[:, :, :, 2 * u : 2 * u + 2]
            nc.scalar.activation(out=dst, in_=src, func=ACT.Copy)
            w1_codes[g, u] = sbuf("w1_codes%d_%d" % (g, u), [P, 2 * P], U32)
            w1_scales[g, u] = sbuf("w1_scales%d_%d" % (g, u), [P, 2 * P], U8)
            quantize(w1_codes[g, u][:], w1_scales[g, u][:], woven[:])

        picked_words = {}
        picked_scales = {}
        quantize_x(0)
        for half in range(2):
            picked_words[0, half] = gather("picked_words0_%d" % half, x_words[0], U32, half)
        quantize_x(1)
        for half in range(2):
            picked_scales[half] = gather("picked_scales%d" % half, x_scales, U8, half)
        for half in range(2):
            quantize_w1(0, half)
            picked_words[1, half] = gather("picked_words1_%d" % half, x_words[1], U32, half, "w1_woven0_%d" % half)
        for u in range(2):
            quantize_w1(1, u)

        banks = {}
        for half in range(2):
            for t in range(PACK):
                banks[t, half] = psum.tile([P, HALF], F32, name="bank%d_%d" % (t, half), tag="bank%d_%d" % (t, half))

        def first_layer(g, t, half):
            columns = slice((t % 2) * P, (t % 2 + 1) * P)
            nc.tensor.matmul_mx(
                out=banks[t, half][:],
                lhsT=w1_codes[g, t // 2][:, columns].bitcast(FP8X4),
                lhsT_scale=w1_scales[g, t // 2][:, columns],
                rhs=picked_words[g, half][:].bitcast(FP8X4),
                rhs_scale=picked_scales[half][PACK * g : P, :],
                start=(g == 0),
                stop=(g == PASSES - 1),
            )

        for t in range(PACK):
            for half in range(2):
                first_layer(0, t, half)
        for t in range(PACK):
            for half in range(2):
                first_layer(1, t, half)

        h = [sbuf("h0", [P, PACK, HALF], F32, "w1_woven1_1"), sbuf("h1", [P, PACK, HALF], F32)]
        sums = [sbuf("sums%d" % half, [P, PACK], F32) for half in range(2)]
        minus_mean = sbuf("minus_mean", [P, PACK, MEAN_PITCH], F32)
        for t in range(PACK):
            nc.vector.tensor_scalar(
                out=h[0][:, t, :], in0=banks[t, 0][:], scalar1=1.0, scalar2=None,
                op0=ALU.mult, op1=ALU.add, accum_out=sums[0][:, t : t + 1],
            )
            nc.scalar.activation(
                out=h[1][:, t, :], in_=banks[t, 1][:], func=ACT.Copy, accum_out=sums[1][:, t : t + 1]
            )
            joiner = nc.vector if t == PACK - 1 else nc.gpsimd
            joiner.tensor_scalar(
                out=minus_mean[:, t, 0:1], in0=sums[0][:, t : t + 1], scalar1=sums[1][:, t : t + 1],
                scalar2=-1.0 / S, op0=ALU.add, op1=ALU.mult,
            )

        w2_woven = sbuf("w2_woven", [P, N, PACK], BF16)
        weave_on_scalar(w2_woven[:], w2_raw[:])
        w2_codes = sbuf("w2_codes", [P, N], U32)
        w2_scales = sbuf("w2_scales", [P, N], U8)
        quantize(w2_codes[:], w2_scales[:], w2_woven[:])

        first = 0
        for n, (width, tiles_on_scalar) in enumerate(Z_PIECES):
            source = h[first // HALF][:, :, first % HALF : first % HALF + width]
            z_rows = sbuf("z_rows%d" % n, [P, PACK, width], BF16)
            for t in range(tiles_on_scalar):
                nc.scalar.activation(
                    out=z_rows[:, t, :], in_=source[:, t, :], func=ACT.Identity, bias=minus_mean[:, t, 0:1]
                )
            for t in range(tiles_on_scalar, PACK):
                nc.vector.tensor_scalar(
                    out=z_rows[:, t, :], in0=source[:, t, :], scalar1=minus_mean[:, t, 0:1], scalar2=None,
                    op0=ALU.add,
                )
            z_woven = sbuf("z_woven%d" % n, [P, width, PACK], BF16)
            weave_on_vector(z_woven[:], z_rows[:])
            z_codes = sbuf("z_codes%d" % n, [P, width], U32)
            z_scales = sbuf("z_scales%d" % n, [P, width], U8)
            quantize(z_codes[:], z_scales[:], z_woven[:])
            product = psum.tile([P, HALF], F32, name="acc%d" % n, tag="bank%d_%d" % (n % PACK, n // PACK))
            nc.tensor.matmul_mx(
                out=product[:, 0:width], lhsT=w2_codes[:].bitcast(FP8X4), lhsT_scale=w2_scales[:],
                rhs=z_codes[:].bitcast(FP8X4), rhs_scale=z_scales[:], start=True, stop=True,
            )
            result = sbuf("result%d" % n, [P, width], F32)
            if n == len(Z_PIECES) - 1:
                nc.vector.tensor_copy(out=result[:], in_=product[:, 0:width])
            else:
                nc.scalar.copy(out=result[:], in_=product[:, 0:width])
            nc.sync.dma_start(out=out[:, first : first + width], in_=result[:])
            first = first + width
